import numpy as np
import ml_dtypes

BF16 = ml_dtypes.bfloat16


def bf(x):
    return np.asarray(x, np.float32).astype(BF16)


def f32(x):
    return np.asarray(x, np.float32)


def f64(x):
    return np.asarray(x).astype(np.float64)


def striped(idx):
    return np.tile(idx.reshape(-1, 16).T, (8, 1))


S, K, M, N, E, Q = 512, 512, 256, 128, 2, 64


def setup_inputs():
    return {"base": bf(np.random.standard_normal((M, S))), "x": bf(np.random.standard_normal((K, N))), "w": bf(np.random.standard_normal((E, K, M)) / np.sqrt(K)), "c": f32(0.2 + 0.8 * np.random.random_sample((1, S))), "offs": striped(np.random.permutation(S)[:N])}


def reference(base, x, w, c, offs):
    idx = offs[:16].T.reshape(-1)
    z = f64(base).copy()
    for e in range(E):
        z[:, idx[e * Q : (e + 1) * Q]] += f64(w)[e].T @ f64(x)[:, e * Q : (e + 1) * Q]
    return z * f64(c)

@@ -1,0 +1,62 @@
+import concourse.mybir as mybir
+from concourse.masks import make_identity
+
+BF16, F32, U16 = mybir.dt.bfloat16, mybir.dt.float32, mybir.dt.uint16
+
+P = 128
+S = 512
+K = 512
+M = 256
+N = 128
+E = 2
+Q = N // E
+KB = K // P
+MB = M // P
+QC = Q // 16
+
+FLOPS = 2 * K * M * N
+
+
+def tile_scatter_matmul_kernel(tc, base, x, w, c, offs, out):
+    nc = tc.nc
+    with (
+        tc.tile_pool(name="held", bufs=1) as held,
+        tc.psum_pool(name="psum", bufs=1) as psum,
+    ):
+        offsets = held.tile([P, N // 16], U16, name="offsets")
+        nc.sync.dma_start(offsets[:], offs)
+
+        ident = held.tile([P, P], BF16, name="ident")
+        make_identity(nc, ident[:])
+
+        base_tiles = [held.tile([P, S], BF16, name="base%d" % mb) for mb in range(MB)]
+        for mb in range(MB):
+            nc.sync.dma_start(base_tiles[mb][:], base[mb * P : (mb + 1) * P, :])
+
+        x_tile = held.tile([P, KB, N], BF16, name="x_tile")
+        nc.scalar.dma_start(x_tile[:], x.rearrange("(kb p) n -> p kb n", p=P))
+        w_tile = held.tile([P, E * KB, M], BF16, name="w_tile")
+        nc.scalar.dma_start(w_tile[:], w.rearrange("e (kb p) m -> p (e kb) m", p=P))
+
+        c_tile = held.tile([P, S], F32, name="c_tile")
+        nc.gpsimd.dma_start(c_tile[:], c.rearrange("o s -> (o s)").partition_broadcast(P))
+
+        windows = [psum.tile([P, S], F32, name="window%d" % mb) for mb in range(MB)]
+        for mb in range(MB):
+            nc.tensor.matmul(windows[mb][:], ident[:], base_tiles[mb][:], start=True, stop=False)
+
+        for mb in range(MB):
+            for e in range(E):
+                for kb in range(KB):
+                    nc.tensor.matmul(
+                        windows[mb][:].indirect(offsets[:, e * QC : (e + 1) * QC]),
+                        w_tile[:, e * KB + kb, mb * P : (mb + 1) * P],
+                        x_tile[:, kb, e * Q : (e + 1) * Q],
+                        start=False,
+                        stop=(e == E - 1 and kb == KB - 1),
+                    )
+
+        for mb in range(MB):
+            scaled = held.tile([P, S], F32, name="scaled%d" % mb)
+            nc.vector.tensor_tensor(scaled[:], windows[mb][:], c_tile[:], mybir.AluOpType.mult)
+            nc.sync.dma_start(out[mb * P : (mb + 1) * P, :], scaled[:])

@@ -26,31 +26,33 @@ def tile_scatter_matmul_kernel(tc, base, x, w, c, offs, out):
         offsets = held.tile([P, N // 16], U16, name="offsets")
         nc.sync.dma_start(offsets[:], offs)
 
-        ident = held.tile([P, P], BF16, name="ident")
-        make_identity(nc, ident[:])
-
+        queues = [nc.sync, nc.scalar]
         base_tiles = [held.tile([P, S], BF16, name="base%d" % mb) for mb in range(MB)]
         for mb in range(MB):
-            nc.sync.dma_start(base_tiles[mb][:], base[mb * P : (mb + 1) * P, :])
+            queues[mb].dma_start(base_tiles[mb][:], base[mb * P : (mb + 1) * P, :])
 
         x_tile = held.tile([P, KB, N], BF16, name="x_tile")
-        nc.scalar.dma_start(x_tile[:], x.rearrange("(kb p) n -> p kb n", p=P))
-        w_tile = held.tile([P, E * KB, M], BF16, name="w_tile")
-        nc.scalar.dma_start(w_tile[:], w.rearrange("e (kb p) m -> p (e kb) m", p=P))
+        nc.scalar.dma_start(x_tile[:], x.rearrange("(p kb) n -> p kb n", kb=KB))
+        w_tiles = [held.tile([P, KB, M], BF16, name="w%d" % e) for e in range(E)]
+        for e in range(E):
+            queues[e].dma_start(w_tiles[e][:], w[e].rearrange("(p kb) m -> p kb m", kb=KB))
 
         c_tile = held.tile([P, S], F32, name="c_tile")
-        nc.gpsimd.dma_start(c_tile[:], c.rearrange("o s -> (o s)").partition_broadcast(P))
+        nc.sync.dma_start(c_tile[:], c.rearrange("o s -> (o s)").partition_broadcast(P))
+
+        ident = held.tile([P, P], BF16, name="ident")
+        make_identity(nc, ident[:])
 
         windows = [psum.tile([P, S], F32, name="window%d" % mb) for mb in range(MB)]
         for mb in range(MB):
             nc.tensor.matmul(windows[mb][:], ident[:], base_tiles[mb][:], start=True, stop=False)
 
-        for mb in range(MB):
-            for e in range(E):
+        for e in range(E):
+            for mb in range(MB):
                 for kb in range(KB):
                     nc.tensor.matmul(
                         windows[mb][:].indirect(offsets[:, e * QC : (e + 1) * QC]),
-                        w_tile[:, e * KB + kb, mb * P : (mb + 1) * P],
+                        w_tiles[e][:, kb, mb * P : (mb + 1) * P],
                         x_tile[:, kb, e * Q : (e + 1) * Q],
                         start=False,
                         stop=(e == E - 1 and kb == KB - 1),
@@ -59,4 +61,4 @@ def tile_scatter_matmul_kernel(tc, base, x, w, c, offs, out):
         for mb in range(MB):
             scaled = held.tile([P, S], F32, name="scaled%d" % mb)
             nc.vector.tensor_tensor(scaled[:], windows[mb][:], c_tile[:], mybir.AluOpType.mult)
-            nc.sync.dma_start(out[mb * P : (mb + 1) * P, :], scaled[:])
+            queues[mb].dma_start(out[mb * P : (mb + 1) * P, :], scaled[:])

@@ -13,6 +13,7 @@ Q = N // E
 KB = K // P
 MB = M // P
 QC = Q // 16
+WARM = 3
 
 FLOPS = 2 * K * M * N
 
@@ -39,6 +40,12 @@ def tile_scatter_matmul_kernel(tc, base, x, w, c, offs, out):
 
         c_tile = held.tile([P, S], F32, name="c_tile")
         nc.sync.dma_start(c_tile[:], c.rearrange("o s -> (o s)").partition_broadcast(P))
+
+        zeros = held.tile([P, S], BF16, name="zeros")
+        nc.vector.memset(zeros[:], 0.0)
+        warm = psum.tile([P, S], F32, name="warm")
+        for i in range(WARM):
+            nc.tensor.matmul(warm[:], zeros[:, 0:P], zeros[:], start=True, stop=True)
 
         ident = held.tile([P, P], BF16, name="ident")
         make_identity(nc, ident[:])

@@ -13,7 +13,7 @@ Q = N // E
 KB = K // P
 MB = M // P
 QC = Q // 16
-WARM = 3
+H = S // 2
 
 FLOPS = 2 * K * M * N
 
@@ -27,6 +27,13 @@ def tile_scatter_matmul_kernel(tc, base, x, w, c, offs, out):
         offsets = held.tile([P, N // 16], U16, name="offsets")
         nc.sync.dma_start(offsets[:], offs)
 
+        c_tile = held.tile([P, S], F32, name="c_tile")
+        nc.scalar.dma_start(c_tile[:], c.rearrange("o s -> (o s)").partition_broadcast(P))
+
+        ident = held.tile([P, P], BF16, name="ident")
+        nc.vector.memset(ident[:], 0.0)
+        make_identity(nc, ident[:], nomemset=True)
+
         queues = [nc.sync, nc.scalar]
         base_tiles = [held.tile([P, S], BF16, name="base%d" % mb) for mb in range(MB)]
         for mb in range(MB):
@@ -37,18 +44,6 @@ def tile_scatter_matmul_kernel(tc, base, x, w, c, offs, out):
         w_tiles = [held.tile([P, KB, M], BF16, name="w%d" % e) for e in range(E)]
         for e in range(E):
             queues[e].dma_start(w_tiles[e][:], w[e].rearrange("(p kb) m -> p kb m", kb=KB))
-
-        c_tile = held.tile([P, S], F32, name="c_tile")
-        nc.sync.dma_start(c_tile[:], c.rearrange("o s -> (o s)").partition_broadcast(P))
-
-        zeros = held.tile([P, S], BF16, name="zeros")
-        nc.vector.memset(zeros[:], 0.0)
-        warm = psum.tile([P, S], F32, name="warm")
-        for i in range(WARM):
-            nc.tensor.matmul(warm[:], zeros[:, 0:P], zeros[:], start=True, stop=True)
-
-        ident = held.tile([P, P], BF16, name="ident")
-        make_identity(nc, ident[:])
 
         windows = [psum.tile([P, S], F32, name="window%d" % mb) for mb in range(MB)]
         for mb in range(MB):
@@ -67,5 +62,7 @@ def tile_scatter_matmul_kernel(tc, base, x, w, c, offs, out):
 
         for mb in range(MB):
             scaled = held.tile([P, S], F32, name="scaled%d" % mb)
-            nc.vector.tensor_tensor(scaled[:], windows[mb][:], c_tile[:], mybir.AluOpType.mult)
-            queues[mb].dma_start(out[mb * P : (mb + 1) * P, :], scaled[:])
+            for h in range(2):
+                cols = slice(h * H, (h + 1) * H)
+                nc.vector.tensor_tensor(scaled[:, cols], windows[mb][:, cols], c_tile[:, cols], mybir.AluOpType.mult)
+                queues[h].dma_start(out[mb * P : (mb + 1) * P, cols], scaled[:, cols])

@@ -27,13 +27,6 @@ def tile_scatter_matmul_kernel(tc, base, x, w, c, offs, out):
         offsets = held.tile([P, N // 16], U16, name="offsets")
         nc.sync.dma_start(offsets[:], offs)
 
-        c_tile = held.tile([P, S], F32, name="c_tile")
-        nc.scalar.dma_start(c_tile[:], c.rearrange("o s -> (o s)").partition_broadcast(P))
-
-        ident = held.tile([P, P], BF16, name="ident")
-        nc.vector.memset(ident[:], 0.0)
-        make_identity(nc, ident[:], nomemset=True)
-
         queues = [nc.sync, nc.scalar]
         base_tiles = [held.tile([P, S], BF16, name="base%d" % mb) for mb in range(MB)]
         for mb in range(MB):
@@ -44,6 +37,12 @@ def tile_scatter_matmul_kernel(tc, base, x, w, c, offs, out):
         w_tiles = [held.tile([P, KB, M], BF16, name="w%d" % e) for e in range(E)]
         for e in range(E):
             queues[e].dma_start(w_tiles[e][:], w[e].rearrange("(p kb) m -> p kb m", kb=KB))
+
+        c_tile = held.tile([P, S], F32, name="c_tile")
+        nc.sync.dma_start(c_tile[:], c.rearrange("o s -> (o s)").partition_broadcast(P))
+
+        ident = held.tile([P, P], BF16, name="ident")
+        make_identity(nc, ident[:])
 
         windows = [psum.tile([P, S], F32, name="window%d" % mb) for mb in range(MB)]
         for mb in range(MB):

@@ -27,6 +27,9 @@ def tile_scatter_matmul_kernel(tc, base, x, w, c, offs, out):
         offsets = held.tile([P, N // 16], U16, name="offsets")
         nc.sync.dma_start(offsets[:], offs)
 
+        c_row = held.tile([1, S], F32, name="c_row")
+        nc.scalar.dma_start(c_row[:], c)
+
         queues = [nc.sync, nc.scalar]
         base_tiles = [held.tile([P, S], BF16, name="base%d" % mb) for mb in range(MB)]
         for mb in range(MB):
@@ -38,11 +41,15 @@ def tile_scatter_matmul_kernel(tc, base, x, w, c, offs, out):
         for e in range(E):
             queues[e].dma_start(w_tiles[e][:], w[e].rearrange("(p kb) m -> p kb m", kb=KB))
 
-        c_tile = held.tile([P, S], F32, name="c_tile")
-        nc.sync.dma_start(c_tile[:], c.rearrange("o s -> (o s)").partition_broadcast(P))
-
         ident = held.tile([P, P], BF16, name="ident")
         make_identity(nc, ident[:])
+
+        ones = held.tile([1, P], F32, name="ones")
+        nc.vector.memset(ones[:], 1.0)
+        c_bank = psum.tile([P, S], F32, name="c_bank")
+        nc.tensor.matmul(c_bank[:], ones[:], c_row[:], start=True, stop=True)
+        c_tile = held.tile([P, S], F32, name="c_tile")
+        nc.vector.tensor_copy(c_tile[:], c_bank[:])
 
         windows = [psum.tile([P, S], F32, name="window%d" % mb) for mb in range(MB)]
         for mb in range(MB):

@@ -14,6 +14,7 @@ KB = K // P
 MB = M // P
 QC = Q // 16
 H = S // 2
+CB = S // P
 
 FLOPS = 2 * K * M * N
 
@@ -27,8 +28,8 @@ def tile_scatter_matmul_kernel(tc, base, x, w, c, offs, out):
         offsets = held.tile([P, N // 16], U16, name="offsets")
         nc.sync.dma_start(offsets[:], offs)
 
-        c_row = held.tile([1, S], F32, name="c_row")
-        nc.scalar.dma_start(c_row[:], c)
+        c_cols = held.tile([P, CB], F32, name="c_cols")
+        nc.scalar.dma_start(c_cols[:], c.rearrange("o (p b) -> p (o b)", b=CB))
 
         queues = [nc.sync, nc.scalar]
         base_tiles = [held.tile([P, S], BF16, name="base%d" % mb) for mb in range(MB)]
@@ -41,15 +42,16 @@ def tile_scatter_matmul_kernel(tc, base, x, w, c, offs, out):
         for e in range(E):
             queues[e].dma_start(w_tiles[e][:], w[e].rearrange("(p kb) m -> p kb m", kb=KB))
 
+        ident_f32 = held.tile([P, P], F32, name="ident_f32")
+        make_identity(nc, ident_f32[:])
         ident = held.tile([P, P], BF16, name="ident")
-        make_identity(nc, ident[:])
+        nc.vector.tensor_copy(ident[:], ident_f32[:])
 
-        ones = held.tile([1, P], F32, name="ones")
-        nc.vector.memset(ones[:], 1.0)
-        c_bank = psum.tile([P, S], F32, name="c_bank")
-        nc.tensor.matmul(c_bank[:], ones[:], c_row[:], start=True, stop=True)
+        c_bank = psum.tile([P, CB, P], F32, name="c_bank")
+        for b in range(CB):
+            nc.tensor.transpose(c_bank[:, b, :], c_cols[:, b : b + 1].to_broadcast([P, P]), ident_f32[:])
         c_tile = held.tile([P, S], F32, name="c_tile")
-        nc.vector.tensor_copy(c_tile[:], c_bank[:])
+        nc.vector.tensor_copy(c_tile[:].rearrange("p (n b) -> p n b", b=CB), c_bank[:].rearrange("p b n -> p n b"))
 
         windows = [psum.tile([P, S], F32, name="window%d" % mb) for mb in range(MB)]
         for mb in range(MB):

@@ -14,6 +14,7 @@ KB = K // P
 MB = M // P
 QC = Q // 16
 H = S // 2
+WARM = 4
 CB = S // P
 
 FLOPS = 2 * K * M * N
@@ -41,6 +42,12 @@ def tile_scatter_matmul_kernel(tc, base, x, w, c, offs, out):
         w_tiles = [held.tile([P, KB, M], BF16, name="w%d" % e) for e in range(E)]
         for e in range(E):
             queues[e].dma_start(w_tiles[e][:], w[e].rearrange("(p kb) m -> p kb m", kb=KB))
+
+        zeros = held.tile([P, S], BF16, name="zeros")
+        nc.vector.memset(zeros[:], 0.0)
+        warm_bank = psum.tile([P, S], F32, name="warm_bank")
+        for i in range(WARM):
+            nc.tensor.matmul(warm_bank[:], zeros[:, 0:P], zeros[:], start=True, stop=True)
 
         ident_f32 = held.tile([P, P], F32, name="ident_f32")
         make_identity(nc, ident_f32[:])

@@ -14,7 +14,7 @@ KB = K // P
 MB = M // P
 QC = Q // 16
 H = S // 2
-WARM = 4
+WARM = 2
 CB = S // P
 
 FLOPS = 2 * K * M * N
@@ -43,11 +43,13 @@ def tile_scatter_matmul_kernel(tc, base, x, w, c, offs, out):
         for e in range(E):
             queues[e].dma_start(w_tiles[e][:], w[e].rearrange("(p kb) m -> p kb m", kb=KB))
 
-        zeros = held.tile([P, S], BF16, name="zeros")
+        zeros = held.tile([P, P], BF16, name="zeros")
         nc.vector.memset(zeros[:], 0.0)
-        warm_bank = psum.tile([P, S], F32, name="warm_bank")
+        warm_bank = psum.tile([P, S // P, P], F32, name="warm_bank")
         for i in range(WARM):
-            nc.tensor.matmul(warm_bank[:], zeros[:, 0:P], zeros[:], start=True, stop=True)
+            nc.tensor.matmul(
+                warm_bank[:], zeros[:], zeros[:].unsqueeze(1).to_broadcast([P, S // P, P]), start=True, stop=True
+            )
 
         ident_f32 = held.tile([P, P], F32, name="ident_f32")
         make_identity(nc, ident_f32[:])

@@ -14,6 +14,7 @@ KB = K // P
 MB = M // P
 QC = Q // 16
 H = S // 2
+W_PIECES = ((0, 0, KB // 2), (0, KB // 2, KB), (1, 0, KB))
 WARM = 2
 CB = S // P
 
@@ -38,10 +39,10 @@ def tile_scatter_matmul_kernel(tc, base, x, w, c, offs, out):
             queues[mb].dma_start(base_tiles[mb][:], base[mb * P : (mb + 1) * P, :])
 
         x_tile = held.tile([P, KB, N], BF16, name="x_tile")
-        nc.scalar.dma_start(x_tile[:], x.rearrange("(p kb) n -> p kb n", kb=KB))
-        w_tiles = [held.tile([P, KB, M], BF16, name="w%d" % e) for e in range(E)]
-        for e in range(E):
-            queues[e].dma_start(w_tiles[e][:], w[e].rearrange("(p kb) m -> p kb m", kb=KB))
+        nc.sync.dma_start(x_tile[:], x.rearrange("(p kb) n -> p kb n", kb=KB))
+        w_tiles = [held.tile([P, kb1 - kb0, M], BF16, name="w%d_%d" % (e, kb0)) for e, kb0, kb1 in W_PIECES]
+        for i, (e, kb0, kb1) in enumerate(W_PIECES):
+            queues[(i + 1) % 2].dma_start(w_tiles[i][:], w[e].rearrange("(p kb) m -> p kb m", kb=KB)[:, kb0:kb1, :])
 
         zeros = held.tile([P, P], BF16, name="zeros")
         nc.vector.memset(zeros[:], 0.0)
@@ -66,12 +67,12 @@ def tile_scatter_matmul_kernel(tc, base, x, w, c, offs, out):
         for mb in range(MB):
             nc.tensor.matmul(windows[mb][:], ident[:], base_tiles[mb][:], start=True, stop=False)
 
-        for e in range(E):
+        for w_tile, (e, kb0, kb1) in zip(w_tiles, W_PIECES):
             for mb in range(MB):
-                for kb in range(KB):
+                for kb in range(kb0, kb1):
                     nc.tensor.matmul(
                         windows[mb][:].indirect(offsets[:, e * QC : (e + 1) * QC]),
-                        w_tiles[e][:, kb, mb * P : (mb + 1) * P],
+                        w_tile[:, kb - kb0, mb * P : (mb + 1) * P],
                         x_tile[:, kb, e * Q : (e + 1) * Q],
                         start=False,
                         stop=(e == E - 1 and kb == KB - 1),

@@ -27,9 +27,6 @@ def tile_scatter_matmul_kernel(tc, base, x, w, c, offs, out):
         tc.tile_pool(name="held", bufs=1) as held,
         tc.psum_pool(name="psum", bufs=1) as psum,
     ):
-        offsets = held.tile([P, N // 16], U16, name="offsets")
-        nc.sync.dma_start(offsets[:], offs)
-
         c_cols = held.tile([P, CB], F32, name="c_cols")
         nc.scalar.dma_start(c_cols[:], c.rearrange("o (p b) -> p (o b)", b=CB))
 
@@ -37,6 +34,9 @@ def tile_scatter_matmul_kernel(tc, base, x, w, c, offs, out):
         base_tiles = [held.tile([P, S], BF16, name="base%d" % mb) for mb in range(MB)]
         for mb in range(MB):
             queues[mb].dma_start(base_tiles[mb][:], base[mb * P : (mb + 1) * P, :])
+
+        offsets = held.tile([P, N // 16], U16, name="offsets")
+        nc.sync.dma_start(offsets[:], offs)
 
         x_tile = held.tile([P, KB, N], BF16, name="x_tile")
         nc.sync.dma_start(x_tile[:], x.rearrange("(p kb) n -> p kb n", kb=KB))

@@ -17,6 +17,7 @@ H = S // 2
 W_PIECES = ((0, 0, KB // 2), (0, KB // 2, KB), (1, 0, KB))
 WARM = 2
 CB = S // P
+ROW_ALIGN = 256
 
 FLOPS = 2 * K * M * N
 
@@ -31,16 +32,18 @@ def tile_scatter_matmul_kernel(tc, base, x, w, c, offs, out):
         nc.scalar.dma_start(c_cols[:], c.rearrange("o (p b) -> p (o b)", b=CB))
 
         queues = [nc.sync, nc.scalar]
-        base_tiles = [held.tile([P, S], BF16, name="base%d" % mb) for mb in range(MB)]
+        base_tiles = [held.tile([P, S], BF16, name="base%d" % mb, align_bytes=ROW_ALIGN) for mb in range(MB)]
         for mb in range(MB):
             queues[mb].dma_start(base_tiles[mb][:], base[mb * P : (mb + 1) * P, :])
 
         offsets = held.tile([P, N // 16], U16, name="offsets")
         nc.sync.dma_start(offsets[:], offs)
 
-        x_tile = held.tile([P, KB, N], BF16, name="x_tile")
+        x_tile = held.tile([P, KB, N], BF16, name="x_tile", align_bytes=ROW_ALIGN)
         nc.sync.dma_start(x_tile[:], x.rearrange("(p kb) n -> p kb n", kb=KB))
-        w_tiles = [held.tile([P, kb1 - kb0, M], BF16, name="w%d_%d" % (e, kb0)) for e, kb0, kb1 in W_PIECES]
+        w_tiles = [
+            held.tile([P, kb1 - kb0, M], BF16, name="w%d_%d" % (e, kb0), align_bytes=ROW_ALIGN) for e, kb0, kb1 in W_PIECES
+        ]
         for i, (e, kb0, kb1) in enumerate(W_PIECES):
             queues[(i + 1) % 2].dma_start(w_tiles[i][:], w[e].rearrange("(p kb) m -> p kb m", kb=KB)[:, kb0:kb1, :])
 
@@ -79,7 +82,7 @@ def tile_scatter_matmul_kernel(tc, base, x, w, c, offs, out):
                     )
 
         for mb in range(MB):
-            scaled = held.tile([P, S], F32, name="scaled%d" % mb)
+            scaled = held.tile([P, S], F32, name="scaled%d" % mb, align_bytes=ROW_ALIGN)
             for h in range(2):
                 cols = slice(h * H, (h + 1) * H)
                 nc.vector.tensor_tensor(scaled[:, cols], windows[mb][:, cols], c_tile[:, cols], mybir.AluOpType.mult)

@@ -31,13 +31,13 @@ def tile_scatter_matmul_kernel(tc, base, x, w, c, offs, out):
         c_cols = held.tile([P, CB], F32, name="c_cols")
         nc.scalar.dma_start(c_cols[:], c.rearrange("o (p b) -> p (o b)", b=CB))
 
+        offsets = held.tile([P, N // 16], U16, name="offsets")
+        nc.sync.dma_start(offsets[:], offs)
+
         queues = [nc.sync, nc.scalar]
         base_tiles = [held.tile([P, S], BF16, name="base%d" % mb, align_bytes=ROW_ALIGN) for mb in range(MB)]
         for mb in range(MB):
             queues[mb].dma_start(base_tiles[mb][:], base[mb * P : (mb + 1) * P, :])
-
-        offsets = held.tile([P, N // 16], U16, name="offsets")
-        nc.sync.dma_start(offsets[:], offs)
 
         x_tile = held.tile([P, KB, N], BF16, name="x_tile", align_bytes=ROW_ALIGN)
         nc.sync.dma_start(x_tile[:], x.rearrange("(p kb) n -> p kb n", kb=KB))

@@ -14,7 +14,7 @@ KB = K // P
 MB = M // P
 QC = Q // 16
 H = S // 2
-W_PIECES = ((0, 0, KB // 2), (0, KB // 2, KB), (1, 0, KB))
+W_PIECES = ((0, 0, KB), (1, 0, KB // 2), (1, KB // 2, KB))
 WARM = 2
 CB = S // P
 ROW_ALIGN = 256
@@ -70,16 +70,18 @@ def tile_scatter_matmul_kernel(tc, base, x, w, c, offs, out):
         for mb in range(MB):
             nc.tensor.matmul(windows[mb][:], ident[:], base_tiles[mb][:], start=True, stop=False)
 
-        for w_tile, (e, kb0, kb1) in zip(w_tiles, W_PIECES):
+        for e in range(E):
             for mb in range(MB):
-                for kb in range(kb0, kb1):
-                    nc.tensor.matmul(
-                        windows[mb][:].indirect(offsets[:, e * QC : (e + 1) * QC]),
-                        w_tile[:, kb - kb0, mb * P : (mb + 1) * P],
-                        x_tile[:, kb, e * Q : (e + 1) * Q],
-                        start=False,
-                        stop=(e == E - 1 and kb == KB - 1),
-                    )
+                for w_tile, (piece_e, kb0, kb1) in zip(w_tiles, W_PIECES):
+                    if piece_e == e:
+                        for kb in range(kb0, kb1):
+                            nc.tensor.matmul(
+                                windows[mb][:].indirect(offsets[:, e * QC : (e + 1) * QC]),
+                                w_tile[:, kb - kb0, mb * P : (mb + 1) * P],
+                                x_tile[:, kb, e * Q : (e + 1) * Q],
+                                start=False,
+                                stop=(e == E - 1 and kb == KB - 1),
+                            )
 
         for mb in range(MB):
             scaled = held.tile([P, S], F32, name="scaled%d" % mb, align_bytes=ROW_ALIGN)

@@ -70,8 +70,8 @@ def tile_scatter_matmul_kernel(tc, base, x, w, c, offs, out):
         for mb in range(MB):
             nc.tensor.matmul(windows[mb][:], ident[:], base_tiles[mb][:], start=True, stop=False)
 
-        for e in range(E):
-            for mb in range(MB):
+        for mb in range(MB):
+            for e in range(E):
                 for w_tile, (piece_e, kb0, kb1) in zip(w_tiles, W_PIECES):
                     if piece_e == e:
                         for kb in range(kb0, kb1):

@@ -37,15 +37,15 @@ def tile_scatter_matmul_kernel(tc, base, x, w, c, offs, out):
         queues = [nc.sync, nc.scalar]
         base_tiles = [held.tile([P, S], BF16, name="base%d" % mb, align_bytes=ROW_ALIGN) for mb in range(MB)]
         for mb in range(MB):
-            queues[mb].dma_start(base_tiles[mb][:], base[mb * P : (mb + 1) * P, :])
+            queues[(mb + 1) % 2].dma_start(base_tiles[mb][:], base[mb * P : (mb + 1) * P, :])
 
         x_tile = held.tile([P, KB, N], BF16, name="x_tile", align_bytes=ROW_ALIGN)
-        nc.sync.dma_start(x_tile[:], x.rearrange("(p kb) n -> p kb n", kb=KB))
+        nc.scalar.dma_start(x_tile[:], x.rearrange("(p kb) n -> p kb n", kb=KB))
         w_tiles = [
             held.tile([P, kb1 - kb0, M], BF16, name="w%d_%d" % (e, kb0), align_bytes=ROW_ALIGN) for e, kb0, kb1 in W_PIECES
         ]
         for i, (e, kb0, kb1) in enumerate(W_PIECES):
-            queues[(i + 1) % 2].dma_start(w_tiles[i][:], w[e].rearrange("(p kb) m -> p kb m", kb=KB)[:, kb0:kb1, :])
+            queues[i % 2].dma_start(w_tiles[i][:], w[e].rearrange("(p kb) m -> p kb m", kb=KB)[:, kb0:kb1, :])
 
         zeros = held.tile([P, P], BF16, name="zeros")
         nc.vector.memset(zeros[:], 0.0)

@@ -13,7 +13,8 @@ Q = N // E
 KB = K // P
 MB = M // P
 QC = Q // 16
-H = S // 2
+CUT = 5 * S // 8
+EPILOGUE = ((0, CUT), (CUT, S))
 W_PIECES = ((0, 0, KB), (1, 0, KB // 2), (1, KB // 2, KB))
 WARM = 2
 CB = S // P
@@ -85,7 +86,7 @@ def tile_scatter_matmul_kernel(tc, base, x, w, c, offs, out):
 
         for mb in range(MB):
             scaled = held.tile([P, S], F32, name="scaled%d" % mb, align_bytes=ROW_ALIGN)
-            for h in range(2):
-                cols = slice(h * H, (h + 1) * H)
+            for queue, (col0, col1) in zip(queues, EPILOGUE):
+                cols = slice(col0, col1)
                 nc.vector.tensor_tensor(scaled[:, cols], windows[mb][:, cols], c_tile[:, cols], mybir.AluOpType.mult)
-                queues[h].dma_start(out[mb * P : (mb + 1) * P, cols], scaled[:, cols])
+                queue.dma_start(out[mb * P : (mb + 1) * P, cols], scaled[:, cols])

@@ -84,9 +84,10 @@ def tile_scatter_matmul_kernel(tc, base, x, w, c, offs, out):
                                 stop=(e == E - 1 and kb == KB - 1),
                             )
 
+        store_queues = [nc.scalar, nc.sync]
         for mb in range(MB):
             scaled = held.tile([P, S], F32, name="scaled%d" % mb, align_bytes=ROW_ALIGN)
-            for queue, (col0, col1) in zip(queues, EPILOGUE):
+            for queue, (col0, col1) in zip(store_queues, EPILOGUE):
                 cols = slice(col0, col1)
                 nc.vector.tensor_tensor(scaled[:, cols], windows[mb][:, cols], c_tile[:, cols], mybir.AluOpType.mult)
                 queue.dma_start(out[mb * P : (mb + 1) * P, cols], scaled[:, cols])

@@ -23,6 +23,16 @@ ROW_ALIGN = 256
 FLOPS = 2 * K * M * N
 
 
+def power_of_two_runs(col0, col1):
+    runs = []
+    for width in (S // 2, S // 4, S // 8):
+        if col1 - col0 >= width:
+            runs.append((col0, col0 + width))
+            col0 += width
+    assert col0 == col1
+    return runs
+
+
 def tile_scatter_matmul_kernel(tc, base, x, w, c, offs, out):
     nc = tc.nc
     with (
@@ -90,4 +100,5 @@ def tile_scatter_matmul_kernel(tc, base, x, w, c, offs, out):
             for queue, (col0, col1) in zip(store_queues, EPILOGUE):
                 cols = slice(col0, col1)
                 nc.vector.tensor_tensor(scaled[:, cols], windows[mb][:, cols], c_tile[:, cols], mybir.AluOpType.mult)
-                queue.dma_start(out[mb * P : (mb + 1) * P, cols], scaled[:, cols])
+                for first, end in power_of_two_runs(col0, col1):
+                    queue.dma_start(out[mb * P : (mb + 1) * P, first:end], scaled[:, first:end])

@@ -14,7 +14,7 @@ KB = K // P
 MB = M // P
 QC = Q // 16
 CUT = 5 * S // 8
-EPILOGUE = ((0, CUT), (CUT, S))
+EPILOGUE = (((0, CUT), (CUT, S)), ((0, S // 2), (S // 2, 3 * S // 4), (3 * S // 4, S)))
 W_PIECES = ((0, 0, KB), (1, 0, KB // 2), (1, KB // 2, KB))
 WARM = 2
 CB = S // P
@@ -97,8 +97,13 @@ def tile_scatter_matmul_kernel(tc, base, x, w, c, offs, out):
         store_queues = [nc.scalar, nc.sync]
         for mb in range(MB):
             scaled = held.tile([P, S], F32, name="scaled%d" % mb, align_bytes=ROW_ALIGN)
-            for queue, (col0, col1) in zip(store_queues, EPILOGUE):
+            for i, (col0, col1) in enumerate(EPILOGUE[mb]):
                 cols = slice(col0, col1)
                 nc.vector.tensor_tensor(scaled[:, cols], windows[mb][:, cols], c_tile[:, cols], mybir.AluOpType.mult)
-                for first, end in power_of_two_runs(col0, col1):
+                if mb == MB - 1 and col1 == S:
+                    middle = (col0 + col1) // 2
+                    stores = [(store_queues[0], col0, middle), (store_queues[1], middle, col1)]
+                else:
+                    stores = [(store_queues[i % 2], first, end) for first, end in power_of_two_runs(col0, col1)]
+                for queue, first, end in stores:
                     queue.dma_start(out[mb * P : (mb + 1) * P, first:end], scaled[:, first:end])

@@ -59,7 +59,7 @@ def tile_scatter_matmul_kernel(tc, base, x, w, c, offs, out):
             queues[i % 2].dma_start(w_tiles[i][:], w[e].rearrange("(p kb) m -> p kb m", kb=KB)[:, kb0:kb1, :])
 
         zeros = held.tile([P, P], BF16, name="zeros")
-        nc.vector.memset(zeros[:], 0.0)
+        nc.gpsimd.memset(zeros[:], 0.0)
         warm_bank = psum.tile([P, S // P, P], F32, name="warm_bank")
         for i in range(WARM):
             nc.tensor.matmul(

import concourse.mybir as mybir
from concourse.masks import make_identity

BF16, F32, U16 = mybir.dt.bfloat16, mybir.dt.float32, mybir.dt.uint16

P = 128
S = 512
K = 512
M = 256
N = 128
E = 2
Q = N // E
KB = K // P
MB = M // P
QC = Q // 16
CUT = 5 * S // 8
EPILOGUE = (((0, CUT), (CUT, S)), ((0, S // 2), (S // 2, 3 * S // 4), (3 * S // 4, S)))
W_PIECES = ((0, 0, KB), (1, 0, KB // 2), (1, KB // 2, KB))
WARM = 2
CB = S // P
ROW_ALIGN = 256

FLOPS = 2 * K * M * N


def power_of_two_runs(col0, col1):
    runs = []
    for width in (S // 2, S // 4, S // 8):
        if col1 - col0 >= width:
            runs.append((col0, col0 + width))
            col0 += width
    assert col0 == col1
    return runs


def tile_scatter_matmul_kernel(tc, base, x, w, c, offs, out):
    nc = tc.nc
    with (
        tc.tile_pool(name="held", bufs=1) as held,
        tc.psum_pool(name="psum", bufs=1) as psum,
    ):
        c_cols = held.tile([P, CB], F32, name="c_cols")
        nc.scalar.dma_start(c_cols[:], c.rearrange("o (p b) -> p (o b)", b=CB))

        offsets = held.tile([P, N // 16], U16, name="offsets")
        nc.sync.dma_start(offsets[:], offs)

        queues = [nc.sync, nc.scalar]
        base_tiles = [held.tile([P, S], BF16, name="base%d" % mb, align_bytes=ROW_ALIGN) for mb in range(MB)]
        for mb in range(MB):
            queues[(mb + 1) % 2].dma_start(base_tiles[mb][:], base[mb * P : (mb + 1) * P, :])

        x_tile = held.tile([P, KB, N], BF16, name="x_tile", align_bytes=ROW_ALIGN)
        nc.scalar.dma_start(x_tile[:], x.rearrange("(p kb) n -> p kb n", kb=KB))
        w_tiles = [
            held.tile([P, kb1 - kb0, M], BF16, name="w%d_%d" % (e, kb0), align_bytes=ROW_ALIGN) for e, kb0, kb1 in W_PIECES
        ]
        for i, (e, kb0, kb1) in enumerate(W_PIECES):
            queues[i % 2].dma_start(w_tiles[i][:], w[e].rearrange("(p kb) m -> p kb m", kb=KB)[:, kb0:kb1, :])

        zeros = held.tile([P, P], BF16, name="zeros")
        nc.gpsimd.memset(zeros[:], 0.0)
        warm_bank = psum.tile([P, S // P, P], F32, name="warm_bank")
        for i in range(WARM):
            nc.tensor.matmul(
                warm_bank[:], zeros[:], zeros[:].unsqueeze(1).to_broadcast([P, S // P, P]), start=True, stop=True
            )

        ident_f32 = held.tile([P, P], F32, name="ident_f32")
        make_identity(nc, ident_f32[:])
        ident = held.tile([P, P], BF16, name="ident")
        nc.vector.tensor_copy(ident[:], ident_f32[:])

        c_bank = psum.tile([P, CB, P], F32, name="c_bank")
        for b in range(CB):
            nc.tensor.transpose(c_bank[:, b, :], c_cols[:, b : b + 1].to_broadcast([P, P]), ident_f32[:])
        c_tile = held.tile([P, S], F32, name="c_tile")
        nc.vector.tensor_copy(c_tile[:].rearrange("p (n b) -> p n b", b=CB), c_bank[:].rearrange("p b n -> p n b"))

        windows = [psum.tile([P, S], F32, name="window%d" % mb) for mb in range(MB)]
        for mb in range(MB):
            nc.tensor.matmul(windows[mb][:], ident[:], base_tiles[mb][:], start=True, stop=False)

        for mb in range(MB):
            for e in range(E):
                for w_tile, (piece_e, kb0, kb1) in zip(w_tiles, W_PIECES):
                    if piece_e == e:
                        for kb in range(kb0, kb1):
                            nc.tensor.matmul(
                                windows[mb][:].indirect(offsets[:, e * QC : (e + 1) * QC]),
                                w_tile[:, kb - kb0, mb * P : (mb + 1) * P],
                                x_tile[:, kb, e * Q : (e + 1) * Q],
                                start=False,
                                stop=(e == E - 1 and kb == KB - 1),
                            )

        store_queues = [nc.scalar, nc.sync]
        for mb in range(MB):
            scaled = held.tile([P, S], F32, name="scaled%d" % mb, align_bytes=ROW_ALIGN)
            for i, (col0, col1) in enumerate(EPILOGUE[mb]):
                cols = slice(col0, col1)
                nc.vector.tensor_tensor(scaled[:, cols], windows[mb][:, cols], c_tile[:, cols], mybir.AluOpType.mult)
                if mb == MB - 1 and col1 == S:
                    middle = (col0 + col1) // 2
                    stores = [(store_queues[0], col0, middle), (store_queues[1], middle, col1)]
                else:
                    stores = [(store_queues[i % 2], first, end) for first, end in power_of_two_runs(col0, col1)]
                for queue, first, end in stores:
                    queue.dma_start(out[mb * P : (mb + 1) * P, first:end], scaled[:, first:end])
